import numpy as np
import ml_dtypes


def mxq(x, axis, fmt="e4m3"):
    dtype, down = {"e4m3": (ml_dtypes.float8_e4m3fn, 7), "e5m2": (ml_dtypes.float8_e5m2, 14)}[fmt]
    v = np.moveaxis(np.asarray(x, np.float32).astype(ml_dtypes.bfloat16).astype(np.float64), axis, -1)
    blocks = v.reshape(v.shape[:-1] + (-1, 32))
    amax = np.abs(blocks).max(-1, keepdims=True)
    byte = np.maximum(np.where(amax > 0, np.frexp(amax)[1] - 1 + 127, 0) - down, 1)
    scale = np.exp2(byte - 127.0)
    codes = (blocks / scale).astype(np.float32).astype(dtype).astype(np.float64)
    return np.moveaxis((codes * scale).reshape(v.shape), -1, axis)


WIDE = False


def mx_kscale(k):
    if not WIDE:
        return np.ones(k)
    levels = np.array([10, -10, 5, -5, 0])
    if k % 512:
        return np.exp2(np.random.permutation(np.resize(levels, k // 32))).repeat(32)
    a = np.empty((k // 512, 16))
    for p in range(k // 512):
        a[p, :8] = np.random.permutation(np.resize(levels, 8))
        for g in range(8):
            far = levels[np.abs(levels - a[p, g]) >= 10]
            a[p, g + 8] = far[np.random.randint(len(far))]
    return np.exp2(a.ravel()).repeat(32)


def f64(x):
    return np.asarray(x).astype(np.float64)


def striped(idx):
    return np.tile(np.asarray(idx).reshape(-1, 16).T, (8, 1)).astype(np.uint16)


def unstriped(offs):
    return offs[:16].T.reshape(-1).astype(np.int64)


E2M1 = np.array([0.0, 0.5, 1.0, 1.5, 2.0, 3.0, 4.0, 6.0, -0.0, -0.5, -1.0, -1.5, -2.0, -3.0, -4.0, -6.0])


def pack_weight(w, fmt):
    k, n = w.shape
    w = f64(np.asarray(w, np.float32).astype(ml_dtypes.bfloat16)).reshape(k // 32, 32, n)
    amax = np.abs(w).max(1)
    if fmt == "e4m3":
        byte = np.frexp(amax)[1] - 1 + 127 - 7
    else:
        mant, ex = np.frexp(amax / 6.0)
        byte = np.where(mant > 0.5, ex, ex - 1) + 127
    byte = np.clip(np.where(amax > 0, byte, 1), 1, 254)
    scaled = (w * np.exp2(127.0 - byte)[:, None, :]).reshape(k, n).astype(np.float32)
    by_word = np.ascontiguousarray(scaled.reshape(k // 512, 128, 4, n).transpose(0, 1, 3, 2))
    if fmt == "e4m3":
        words = by_word.astype(ml_dtypes.float8_e4m3fn).view(np.uint8)
    else:
        c = by_word.astype(ml_dtypes.float4_e2m1fn).view(np.uint8) & 0xF
        words = (c[..., 0::2] | (c[..., 1::2] << 4)).reshape(k // 512, 128, 2 * n)
    return np.ascontiguousarray(words), np.ascontiguousarray(byte.astype(np.uint8).reshape(k // 512, 16, n))


def unpack_weight(words, scales, fmt):
    g, _, n = scales.shape
    words = np.ascontiguousarray(words).reshape(g, 128, n, -1)
    if fmt == "e4m3":
        vals = words.view(ml_dtypes.float8_e4m3fn).astype(np.float64)
    else:
        nib = np.empty((g, 128, n, 4), np.uint8)
        nib[..., 0::2] = words & 0xF
        nib[..., 1::2] = words >> 4
        vals = E2M1[nib]
    vals = vals * np.repeat(np.exp2(scales.astype(np.float64) - 127.0), 8, axis=1)[..., None]
    return vals.transpose(0, 1, 3, 2).reshape(g * 512, n)


def sigmoid(v):
    return 1.0 / (1.0 + np.exp(-v))


B, N, T, D, NQ = 1, 512, 2048, 1024, 128


def setup_inputs():
    n = np.random.standard_normal
    idx = np.random.permutation(T)[:B * N]
    s = mx_kscale(D)[:, None]
    kp = pack_weight(n((D, T)) / s, "e2m1")
    return {
        "qT": (n((B, D, NQ)) * s * (1.00 / np.sqrt(D))).astype(np.float32),
        "k_words": np.ascontiguousarray(kp[0].reshape(1, 2, 128, T, 2).transpose(0, 2, 3, 1, 4)).reshape(1, 128, T, 4),
        "k_scales": kp[1],
        "c1": (-np.random.uniform(0.2, 1.0, (B, NQ, 1))).astype(np.float32),
        "c2": (np.random.uniform(0.2, 1.0, (B, NQ, 1))).astype(np.float32),
        "offs": striped(idx),
    }


def reference(qT, k_words, k_scales, c1, c2, offs):
    idx = unstriped(offs)
    pick = lambda x, which: x[:, which].reshape(x.shape[0], B, -1).transpose(1, 0, 2)
    k = unpack_weight(k_words.reshape(1, 128, T, 2, 2).transpose(0, 3, 1, 2, 4).reshape(2, 128, 2 * T), k_scales, "e2m1")
    kg = pick(k, idx)
    qq = mxq(f64(qT), 1, "e4m3")
    a = qq.transpose(0, 2, 1) @ kg
    y = sigmoid(f64(c2) - a) - sigmoid(f64(c1) - a)
    return y

@@ -1,0 +1,132 @@
+from contextlib import ExitStack
+
+import concourse.mybir as mybir
+
+D, T, N, NQ = 1024, 2048, 512, 128
+FLOPS = 2 * D * N * NQ
+
+F32 = mybir.dt.float32
+BF16 = mybir.dt.bfloat16
+I32 = mybir.dt.int32
+U32 = mybir.dt.uint32
+U16 = mybir.dt.uint16
+U8 = mybir.dt.uint8
+FP8X4 = mybir.dt.float8_e4m3fn_x4
+FP4X4 = mybir.dt.float4_e2m1fn_x4
+SIGMOID = mybir.ActivationFunctionType.Sigmoid
+SUBTRACT = mybir.AluOpType.subtract
+
+P = 128
+PACK = 4
+K_PASS = P * PACK
+PASSES = D // K_PASS
+HALF = N // 2
+GROUP = 128
+
+
+def tile_attend_link_ordinal_topk_kernel(tc, qT, k_words, k_scales, c1, c2, offs, out):
+    nc = tc.nc
+    with ExitStack() as ctx:
+        pool = ctx.enter_context(tc.tile_pool(name="held", bufs=1))
+        psum = ctx.enter_context(tc.psum_pool(name="psum", bufs=1))
+
+        offsets = pool.tile([P, N // 16], U16, name="offsets")
+        nc.sync.dma_start(offsets[:], offs)
+
+        scale_rows = pool.tile([P, T], U8, name="scale_rows", align_bytes=64)
+        nc.vector.memset(scale_rows[:].bitcast(I32), 0)
+        nc.scalar.dma_start(
+            out=scale_rows[0:P:4, :].bitcast(I32),
+            in_=k_scales.bitcast(I32).rearrange("o f t -> f o t"),
+        )
+        key_scales = pool.tile([P, PASSES * N], U8, name="key_scales", align_bytes=64)
+        nc.vector.memset(key_scales[:].bitcast(I32), 0)
+        warm = pool.tile([P, 1], F32, name="warm")
+        nc.vector.memset(warm[:], 0.0)
+        warmed = pool.tile([P, 1], F32, name="warmed")
+        nc.scalar.activation(out=warmed[:], in_=warm[:], func=SIGMOID)
+
+        lower = pool.tile([P, 1], F32, name="lower")
+        upper = pool.tile([P, 1], F32, name="upper")
+
+        q_raw = [pool.tile([P, PACK, NQ], F32, name="q_raw%d" % o) for o in range(PASSES)]
+        words = pool.tile([P, T], I32, name="words", align_bytes=64)
+
+        def load_q(o):
+            rows = qT[0, o * K_PASS : (o + 1) * K_PASS, :]
+            nc.sync.dma_start(out=q_raw[o][:], in_=rows.rearrange("(p j) n -> p j n", j=PACK))
+
+        load_q(0)
+        nc.sync.dma_start(out=words[:], in_=k_words[0].rearrange("g t b -> g (t b)").bitcast(I32))
+        load_q(1)
+        nc.sync.dma_start(out=upper[:], in_=c2[0])
+        nc.sync.dma_start(out=lower[:], in_=c1[0])
+
+        listed_rows = pool.tile([P, N], U8, name="listed_rows", align_bytes=64)
+        nc.vector.tensor_copy(listed_rows[:], scale_rows[:].indirect(offsets[:]))
+        for quad in range(4):
+            nc.scalar.dma_start(
+                out=key_scales[32 * quad : 32 * quad + 4, :].bitcast(I32).rearrange("p (o n) -> p o n", o=PASSES),
+                in_=listed_rows[32 * quad : 32 * quad + 32 : 4, :].bitcast(I32),
+            )
+
+        q_codes = [pool.tile([P, NQ], U32, name="q_codes%d" % o, align_bytes=64) for o in range(PASSES)]
+        q_scales = [pool.tile([P, NQ], U8, name="q_scales%d" % o, align_bytes=64) for o in range(PASSES)]
+
+        def quantize_q(o):
+            grouped = pool.tile([P, NQ, PACK], BF16, name="q_grouped%d" % o, align_bytes=64)
+            nc.scalar.copy(
+                out=grouped[:].rearrange("p (c i) t -> p c t i", i=4),
+                in_=q_raw[o][:].rearrange("p t (c i) -> p c t i", i=4),
+            )
+            nc.vector.quantize_mx(
+                out=q_codes[o][:].bitcast(FP8X4),
+                scales=q_scales[o][:],
+                in_=grouped[:].rearrange("p n t -> p (n t)"),
+            )
+
+        pairs = [pool.tile([P, HALF], U32, name="pairs%d" % h, align_bytes=64) for h in range(2)]
+        key_codes = [pool.tile([P, PASSES, HALF], U16, name="key_codes%d" % h, align_bytes=64) for h in range(2)]
+
+        def gather_words(h):
+            cols = HALF // 16
+            nc.vector.tensor_copy(pairs[h][:], words[:].bitcast(U32).indirect(offsets[:, h * cols : (h + 1) * cols]))
+
+        def part_words(h):
+            nc.vector.tensor_copy(key_codes[h][:], pairs[h][:].bitcast(U16).rearrange("p (n o) -> p o n", o=PASSES))
+
+        def score(h):
+            acc = psum.tile([P, HALF], F32, name="acc%d" % h)
+            for g0 in range(0, HALF, GROUP):
+                for o in range(PASSES):
+                    s0 = o * N + h * HALF + g0
+                    nc.tensor.matmul_mx(
+                        out=acc[:, g0 : g0 + GROUP],
+                        lhsT=q_codes[o][:].bitcast(FP8X4),
+                        lhsT_scale=q_scales[o][:],
+                        rhs=key_codes[h][:, o, g0 : g0 + GROUP].bitcast(FP4X4),
+                        rhs_scale=key_scales[:, s0 : s0 + GROUP],
+                        start=(o == 0),
+                        stop=(o == PASSES - 1),
+                    )
+            below_upper = pool.tile([P, HALF], F32, name="below_upper%d" % h)
+            below_lower = pool.tile([P, HALF], F32, name="below_lower%d" % h)
+            nc.scalar.activation(out=below_upper[:], in_=acc[:], func=SIGMOID, bias=upper[:], scale=-1.0)
+            nc.scalar.activation(out=below_lower[:], in_=acc[:], func=SIGMOID, bias=lower[:], scale=-1.0)
+            return below_upper, below_lower
+
+        def finish(h, below_upper, below_lower):
+            result = pool.tile([P, HALF], F32, name="result%d" % h)
+            nc.vector.tensor_tensor(out=result[:], in0=below_upper[:], in1=below_lower[:], op=SUBTRACT)
+            nc.sync.dma_start(out=out[0, :, h * HALF : (h + 1) * HALF], in_=result[:])
+
+        quantize_q(0)
+        gather_words(0)
+        part_words(0)
+        gather_words(1)
+        quantize_q(1)
+        part_words(1)
+        first = score(0)
+        second = score(1)
+        finish(0, *first)
+        finish(1, *second)

@@ -34,20 +34,22 @@ def tile_attend_link_ordinal_topk_kernel(tc, qT, k_words, k_scales, c1, c2, offs
         nc.sync.dma_start(offsets[:], offs)
 
         scale_rows = pool.tile([P, T], U8, name="scale_rows", align_bytes=64)
-        nc.vector.memset(scale_rows[:].bitcast(I32), 0)
         nc.scalar.dma_start(
-            out=scale_rows[0:P:4, :].bitcast(I32),
+            out=scale_rows[0:32, :].bitcast(I32),
             in_=k_scales.bitcast(I32).rearrange("o f t -> f o t"),
         )
+        lower = pool.tile([P, 1], F32, name="lower")
+        upper = pool.tile([P, 1], F32, name="upper")
+        nc.scalar.dma_start(out=upper[:], in_=c2[0])
+        nc.scalar.dma_start(out=lower[:], in_=c1[0])
+        nc.vector.memset(scale_rows[32:64, :].bitcast(I32), 0)
+        nc.vector.memset(scale_rows[64:P, :].bitcast(I32), 0)
         key_scales = pool.tile([P, PASSES * N], U8, name="key_scales", align_bytes=64)
         nc.vector.memset(key_scales[:].bitcast(I32), 0)
         warm = pool.tile([P, 1], F32, name="warm")
         nc.vector.memset(warm[:], 0.0)
         warmed = pool.tile([P, 1], F32, name="warmed")
         nc.scalar.activation(out=warmed[:], in_=warm[:], func=SIGMOID)
-
-        lower = pool.tile([P, 1], F32, name="lower")
-        upper = pool.tile([P, 1], F32, name="upper")
 
         q_raw = [pool.tile([P, PACK, NQ], F32, name="q_raw%d" % o) for o in range(PASSES)]
         words = pool.tile([P, T], I32, name="words", align_bytes=64)
@@ -56,18 +58,16 @@ def tile_attend_link_ordinal_topk_kernel(tc, qT, k_words, k_scales, c1, c2, offs
             rows = qT[0, o * K_PASS : (o + 1) * K_PASS, :]
             nc.sync.dma_start(out=q_raw[o][:], in_=rows.rearrange("(p j) n -> p j n", j=PACK))
 
-        load_q(0)
         nc.sync.dma_start(out=words[:], in_=k_words[0].rearrange("g t b -> g (t b)").bitcast(I32))
+        load_q(0)
         load_q(1)
-        nc.sync.dma_start(out=upper[:], in_=c2[0])
-        nc.sync.dma_start(out=lower[:], in_=c1[0])
 
         listed_rows = pool.tile([P, N], U8, name="listed_rows", align_bytes=64)
         nc.vector.tensor_copy(listed_rows[:], scale_rows[:].indirect(offsets[:]))
         for quad in range(4):
             nc.scalar.dma_start(
                 out=key_scales[32 * quad : 32 * quad + 4, :].bitcast(I32).rearrange("p (o n) -> p o n", o=PASSES),
-                in_=listed_rows[32 * quad : 32 * quad + 32 : 4, :].bitcast(I32),
+                in_=listed_rows[8 * quad : 8 * quad + 8, :].bitcast(I32),
             )
 
         q_codes = [pool.tile([P, NQ], U32, name="q_codes%d" % o, align_bytes=64) for o in range(PASSES)]
@@ -95,38 +95,39 @@ def tile_attend_link_ordinal_topk_kernel(tc, qT, k_words, k_scales, c1, c2, offs
         def part_words(h):
             nc.vector.tensor_copy(key_codes[h][:], pairs[h][:].bitcast(U16).rearrange("p (n o) -> p o n", o=PASSES))
 
-        def score(h):
-            acc = psum.tile([P, HALF], F32, name="acc%d" % h)
-            for g0 in range(0, HALF, GROUP):
-                for o in range(PASSES):
-                    s0 = o * N + h * HALF + g0
-                    nc.tensor.matmul_mx(
-                        out=acc[:, g0 : g0 + GROUP],
-                        lhsT=q_codes[o][:].bitcast(FP8X4),
-                        lhsT_scale=q_scales[o][:],
-                        rhs=key_codes[h][:, o, g0 : g0 + GROUP].bitcast(FP4X4),
-                        rhs_scale=key_scales[:, s0 : s0 + GROUP],
-                        start=(o == 0),
-                        stop=(o == PASSES - 1),
-                    )
-            below_upper = pool.tile([P, HALF], F32, name="below_upper%d" % h)
-            below_lower = pool.tile([P, HALF], F32, name="below_lower%d" % h)
-            nc.scalar.activation(out=below_upper[:], in_=acc[:], func=SIGMOID, bias=upper[:], scale=-1.0)
-            nc.scalar.activation(out=below_lower[:], in_=acc[:], func=SIGMOID, bias=lower[:], scale=-1.0)
-            return below_upper, below_lower
+        accs = [psum.tile([P, GROUP], F32, name="acc%d" % g) for g in range(N // GROUP)]
 
-        def finish(h, below_upper, below_lower):
-            result = pool.tile([P, HALF], F32, name="result%d" % h)
+        def multiply(g, o):
+            h, g0 = divmod(g * GROUP, HALF)
+            s0 = o * N + g * GROUP
+            nc.tensor.matmul_mx(
+                out=accs[g][:],
+                lhsT=q_codes[o][:].bitcast(FP8X4),
+                lhsT_scale=q_scales[o][:],
+                rhs=key_codes[h][:, o, g0 : g0 + GROUP].bitcast(FP4X4),
+                rhs_scale=key_scales[:, s0 : s0 + GROUP],
+                start=(o == 0),
+                stop=(o == PASSES - 1),
+            )
+
+        def link(g):
+            below_upper = pool.tile([P, GROUP], F32, name="below_upper%d" % g)
+            below_lower = pool.tile([P, GROUP], F32, name="below_lower%d" % g)
+            nc.scalar.activation(out=below_upper[:], in_=accs[g][:], func=SIGMOID, bias=upper[:], scale=-1.0)
+            nc.scalar.activation(out=below_lower[:], in_=accs[g][:], func=SIGMOID, bias=lower[:], scale=-1.0)
+            result = pool.tile([P, GROUP], F32, name="result%d" % g)
             nc.vector.tensor_tensor(out=result[:], in0=below_upper[:], in1=below_lower[:], op=SUBTRACT)
-            nc.sync.dma_start(out=out[0, :, h * HALF : (h + 1) * HALF], in_=result[:])
+            nc.sync.dma_start(out=out[0, :, g * GROUP : (g + 1) * GROUP], in_=result[:])
 
-        quantize_q(0)
         gather_words(0)
-        part_words(0)
         gather_words(1)
+        part_words(0)
+        quantize_q(0)
         quantize_q(1)
         part_words(1)
-        first = score(0)
-        second = score(1)
-        finish(0, *first)
-        finish(1, *second)
+        for h in range(2):
+            for o in range(PASSES):
+                for g in (2 * h, 2 * h + 1):
+                    multiply(g, o)
+        for g in range(N // GROUP):
+            link(g)

@@ -31,17 +31,22 @@ def tile_attend_link_ordinal_topk_kernel(tc, qT, k_words, k_scales, c1, c2, offs
         psum = ctx.enter_context(tc.psum_pool(name="psum", bufs=1))
 
         offsets = pool.tile([P, N // 16], U16, name="offsets")
-        nc.sync.dma_start(offsets[:], offs)
-
         scale_rows = pool.tile([P, T], U8, name="scale_rows", align_bytes=64)
-        nc.scalar.dma_start(
+        nc.sync.dma_start(
             out=scale_rows[0:32, :].bitcast(I32),
             in_=k_scales.bitcast(I32).rearrange("o f t -> f o t"),
         )
+        nc.sync.dma_start(offsets[:], offs)
+        q_raw = [pool.tile([P, PACK, NQ], F32, name="q_raw%d" % o) for o in range(PASSES)]
+        words = pool.tile([P, T], I32, name="words", align_bytes=64)
+        nc.sync.dma_start(out=words[:], in_=k_words[0].rearrange("g t b -> g (t b)").bitcast(I32))
+        for o in range(PASSES):
+            rows = qT[0, o * K_PASS : (o + 1) * K_PASS, :]
+            nc.sync.dma_start(out=q_raw[o][:], in_=rows.rearrange("(p j) n -> p j n", j=PACK))
         lower = pool.tile([P, 1], F32, name="lower")
         upper = pool.tile([P, 1], F32, name="upper")
-        nc.scalar.dma_start(out=upper[:], in_=c2[0])
-        nc.scalar.dma_start(out=lower[:], in_=c1[0])
+        nc.sync.dma_start(out=upper[:], in_=c2[0])
+        nc.sync.dma_start(out=lower[:], in_=c1[0])
         nc.vector.memset(scale_rows[32:64, :].bitcast(I32), 0)
         nc.vector.memset(scale_rows[64:P, :].bitcast(I32), 0)
         key_scales = pool.tile([P, PASSES * N], U8, name="key_scales", align_bytes=64)
@@ -50,17 +55,6 @@ def tile_attend_link_ordinal_topk_kernel(tc, qT, k_words, k_scales, c1, c2, offs
         nc.vector.memset(warm[:], 0.0)
         warmed = pool.tile([P, 1], F32, name="warmed")
         nc.scalar.activation(out=warmed[:], in_=warm[:], func=SIGMOID)
-
-        q_raw = [pool.tile([P, PACK, NQ], F32, name="q_raw%d" % o) for o in range(PASSES)]
-        words = pool.tile([P, T], I32, name="words", align_bytes=64)
-
-        def load_q(o):
-            rows = qT[0, o * K_PASS : (o + 1) * K_PASS, :]
-            nc.sync.dma_start(out=q_raw[o][:], in_=rows.rearrange("(p j) n -> p j n", j=PACK))
-
-        nc.sync.dma_start(out=words[:], in_=k_words[0].rearrange("g t b -> g (t b)").bitcast(I32))
-        load_q(0)
-        load_q(1)
 
         listed_rows = pool.tile([P, N], U8, name="listed_rows", align_bytes=64)
         nc.vector.tensor_copy(listed_rows[:], scale_rows[:].indirect(offsets[:]))
@@ -125,9 +119,8 @@ def tile_attend_link_ordinal_topk_kernel(tc, qT, k_words, k_scales, c1, c2, offs
         quantize_q(0)
         quantize_q(1)
         part_words(1)
-        for h in range(2):
+        for g in range(N // GROUP):
             for o in range(PASSES):
-                for g in (2 * h, 2 * h + 1):
-                    multiply(g, o)
+                multiply(g, o)
         for g in range(N // GROUP):
             link(g)

@@ -22,12 +22,14 @@ K_PASS = P * PACK
 PASSES = D // K_PASS
 HALF = N // 2
 GROUP = 128
+VECTOR_COLS = 80
 
 
 def tile_attend_link_ordinal_topk_kernel(tc, qT, k_words, k_scales, c1, c2, offs, out):
     nc = tc.nc
     with ExitStack() as ctx:
         pool = ctx.enter_context(tc.tile_pool(name="held", bufs=1))
+        reused = ctx.enter_context(tc.tile_pool(name="reused", bufs=1))
         psum = ctx.enter_context(tc.psum_pool(name="psum", bufs=1))
 
         offsets = pool.tile([P, N // 16], U16, name="offsets")
@@ -37,7 +39,10 @@ def tile_attend_link_ordinal_topk_kernel(tc, qT, k_words, k_scales, c1, c2, offs
             in_=k_scales.bitcast(I32).rearrange("o f t -> f o t"),
         )
         nc.sync.dma_start(offsets[:], offs)
-        q_raw = [pool.tile([P, PACK, NQ], F32, name="q_raw%d" % o) for o in range(PASSES)]
+        q_raw = [
+            pool.tile([P, PACK, NQ], F32, name="q_raw0"),
+            reused.tile([P, PACK, NQ], F32, name="q_raw1", offset=0, align_bytes=64),
+        ]
         words = pool.tile([P, T], I32, name="words", align_bytes=64)
         nc.sync.dma_start(out=words[:], in_=k_words[0].rearrange("g t b -> g (t b)").bitcast(I32))
         for o in range(PASSES):
@@ -67,38 +72,45 @@ def tile_attend_link_ordinal_topk_kernel(tc, qT, k_words, k_scales, c1, c2, offs
         q_codes = [pool.tile([P, NQ], U32, name="q_codes%d" % o, align_bytes=64) for o in range(PASSES)]
         q_scales = [pool.tile([P, NQ], U8, name="q_scales%d" % o, align_bytes=64) for o in range(PASSES)]
 
-        def quantize_q(o):
-            grouped = pool.tile([P, NQ, PACK], BF16, name="q_grouped%d" % o, align_bytes=64)
-            nc.scalar.copy(
-                out=grouped[:].rearrange("p (c i) t -> p c t i", i=4),
-                in_=q_raw[o][:].rearrange("p t (c i) -> p c t i", i=4),
+        grouped = [pool.tile([P, NQ, PACK], BF16, name="q_grouped%d" % o, align_bytes=64) for o in range(PASSES)]
+
+        def cast_q(copy, o, c0, c1):
+            copy(
+                out=grouped[o][:, c0:c1, :].rearrange("p (c i) t -> p c t i", i=4),
+                in_=q_raw[o][:, :, c0:c1].rearrange("p t (c i) -> p c t i", i=4),
             )
+
+        def quantize_q(o):
             nc.vector.quantize_mx(
                 out=q_codes[o][:].bitcast(FP8X4),
                 scales=q_scales[o][:],
-                in_=grouped[:].rearrange("p n t -> p (n t)"),
+                in_=grouped[o][:].rearrange("p n t -> p (n t)"),
             )
 
         pairs = [pool.tile([P, HALF], U32, name="pairs%d" % h, align_bytes=64) for h in range(2)]
-        key_codes = [pool.tile([P, PASSES, HALF], U16, name="key_codes%d" % h, align_bytes=64) for h in range(2)]
+        key_codes = [pool.tile([P, PASSES, GROUP], U16, name="key_codes0", align_bytes=64)] + [
+            reused.tile([P, PASSES, GROUP], U16, name="key_codes%d" % g, offset=(g - 1) * GROUP * 4, align_bytes=64)
+            for g in range(1, N // GROUP)
+        ]
 
         def gather_words(h):
             cols = HALF // 16
             nc.vector.tensor_copy(pairs[h][:], words[:].bitcast(U32).indirect(offsets[:, h * cols : (h + 1) * cols]))
 
-        def part_words(h):
-            nc.vector.tensor_copy(key_codes[h][:], pairs[h][:].bitcast(U16).rearrange("p (n o) -> p o n", o=PASSES))
+        def part_words(g):
+            h, g0 = divmod(g * GROUP, HALF)
+            halves = pairs[h][:, g0 : g0 + GROUP].bitcast(U16)
+            nc.vector.tensor_copy(key_codes[g][:], halves.rearrange("p (n o) -> p o n", o=PASSES))
 
         accs = [psum.tile([P, GROUP], F32, name="acc%d" % g) for g in range(N // GROUP)]
 
         def multiply(g, o):
-            h, g0 = divmod(g * GROUP, HALF)
             s0 = o * N + g * GROUP
             nc.tensor.matmul_mx(
                 out=accs[g][:],
                 lhsT=q_codes[o][:].bitcast(FP8X4),
                 lhsT_scale=q_scales[o][:],
-                rhs=key_codes[h][:, o, g0 : g0 + GROUP].bitcast(FP4X4),
+                rhs=key_codes[g][:, o, :].bitcast(FP4X4),
                 rhs_scale=key_scales[:, s0 : s0 + GROUP],
                 start=(o == 0),
                 stop=(o == PASSES - 1),
@@ -115,10 +127,14 @@ def tile_attend_link_ordinal_topk_kernel(tc, qT, k_words, k_scales, c1, c2, offs
 
         gather_words(0)
         gather_words(1)
+        cast_q(nc.scalar.copy, 0, 0, NQ)
+        cast_q(nc.vector.tensor_copy, 1, 0, VECTOR_COLS)
+        cast_q(nc.scalar.copy, 1, VECTOR_COLS, NQ)
         part_words(0)
         quantize_q(0)
         quantize_q(1)
-        part_words(1)
+        for g in range(1, N // GROUP):
+            part_words(g)
         for g in range(N // GROUP):
             for o in range(PASSES):
                 multiply(g, o)

@@ -22,7 +22,8 @@ K_PASS = P * PACK
 PASSES = D // K_PASS
 HALF = N // 2
 GROUP = 128
-VECTOR_COLS = 80
+VECTOR_COLS = 48
+Q_BYTES = PACK * NQ * 4
 
 
 def tile_attend_link_ordinal_topk_kernel(tc, qT, k_words, k_scales, c1, c2, offs, out):
@@ -40,7 +41,7 @@ def tile_attend_link_ordinal_topk_kernel(tc, qT, k_words, k_scales, c1, c2, offs
         )
         nc.sync.dma_start(offsets[:], offs)
         q_raw = [
-            pool.tile([P, PACK, NQ], F32, name="q_raw0"),
+            reused.tile([P, PACK, NQ], F32, name="q_raw0", offset=Q_BYTES, align_bytes=64),
             reused.tile([P, PACK, NQ], F32, name="q_raw1", offset=0, align_bytes=64),
         ]
         words = pool.tile([P, T], I32, name="words", align_bytes=64)
@@ -48,10 +49,10 @@ def tile_attend_link_ordinal_topk_kernel(tc, qT, k_words, k_scales, c1, c2, offs
         for o in range(PASSES):
             rows = qT[0, o * K_PASS : (o + 1) * K_PASS, :]
             nc.sync.dma_start(out=q_raw[o][:], in_=rows.rearrange("(p j) n -> p j n", j=PACK))
-        lower = pool.tile([P, 1], F32, name="lower")
-        upper = pool.tile([P, 1], F32, name="upper")
-        nc.sync.dma_start(out=upper[:], in_=c2[0])
-        nc.sync.dma_start(out=lower[:], in_=c1[0])
+        threshold_rows = pool.tile([P, 32], F32, name="threshold_rows", align_bytes=64)
+        nc.vector.memset(threshold_rows[:], 0.0)
+        for r, c in enumerate((c2, c1)):
+            nc.scalar.dma_start(out=threshold_rows[r:P:32, :], in_=c[0].rearrange("(q j) o -> q (j o)", j=32))
         nc.vector.memset(scale_rows[32:64, :].bitcast(I32), 0)
         nc.vector.memset(scale_rows[64:P, :].bitcast(I32), 0)
         key_scales = pool.tile([P, PASSES * N], U8, name="key_scales", align_bytes=64)
@@ -61,10 +62,12 @@ def tile_attend_link_ordinal_topk_kernel(tc, qT, k_words, k_scales, c1, c2, offs
         warmed = pool.tile([P, 1], F32, name="warmed")
         nc.scalar.activation(out=warmed[:], in_=warm[:], func=SIGMOID)
 
+        thresholds = reused.tile([P, 32], F32, name="thresholds", offset=3 * GROUP * 4, align_bytes=64)
+        upper, lower = thresholds[:, 0:1], thresholds[:, 1:2]
         listed_rows = pool.tile([P, N], U8, name="listed_rows", align_bytes=64)
         nc.vector.tensor_copy(listed_rows[:], scale_rows[:].indirect(offsets[:]))
         for quad in range(4):
-            nc.scalar.dma_start(
+            (nc.sync if quad % 2 == 0 else nc.scalar).dma_start(
                 out=key_scales[32 * quad : 32 * quad + 4, :].bitcast(I32).rearrange("p (o n) -> p o n", o=PASSES),
                 in_=listed_rows[8 * quad : 8 * quad + 8, :].bitcast(I32),
             )
@@ -87,20 +90,15 @@ def tile_attend_link_ordinal_topk_kernel(tc, qT, k_words, k_scales, c1, c2, offs
                 in_=grouped[o][:].rearrange("p n t -> p (n t)"),
             )
 
-        pairs = [pool.tile([P, HALF], U32, name="pairs%d" % h, align_bytes=64) for h in range(2)]
-        key_codes = [pool.tile([P, PASSES, GROUP], U16, name="key_codes0", align_bytes=64)] + [
-            reused.tile([P, PASSES, GROUP], U16, name="key_codes%d" % g, offset=(g - 1) * GROUP * 4, align_bytes=64)
-            for g in range(1, N // GROUP)
+        pairs = pool.tile([P, N], U32, name="pairs", align_bytes=64)
+        pieces = [(g * GROUP, (g + 1) * GROUP, (g - 1) * GROUP * 4 if g else Q_BYTES) for g in range(N // GROUP)]
+        key_codes = [
+            reused.tile([P, PASSES, b - a], U16, name="key_codes%d" % a, offset=at, align_bytes=64) for a, b, at in pieces
         ]
 
-        def gather_words(h):
-            cols = HALF // 16
-            nc.vector.tensor_copy(pairs[h][:], words[:].bitcast(U32).indirect(offsets[:, h * cols : (h + 1) * cols]))
-
-        def part_words(g):
-            h, g0 = divmod(g * GROUP, HALF)
-            halves = pairs[h][:, g0 : g0 + GROUP].bitcast(U16)
-            nc.vector.tensor_copy(key_codes[g][:], halves.rearrange("p (n o) -> p o n", o=PASSES))
+        def part_words(i):
+            a, b = pieces[i][:2]
+            nc.vector.tensor_copy(key_codes[i][:], pairs[:, a:b].bitcast(U16).rearrange("p (n o) -> p o n", o=PASSES))
 
         accs = [psum.tile([P, GROUP], F32, name="acc%d" % g) for g in range(N // GROUP)]
 
@@ -119,22 +117,23 @@ def tile_attend_link_ordinal_topk_kernel(tc, qT, k_words, k_scales, c1, c2, offs
         def link(g):
             below_upper = pool.tile([P, GROUP], F32, name="below_upper%d" % g)
             below_lower = pool.tile([P, GROUP], F32, name="below_lower%d" % g)
-            nc.scalar.activation(out=below_upper[:], in_=accs[g][:], func=SIGMOID, bias=upper[:], scale=-1.0)
-            nc.scalar.activation(out=below_lower[:], in_=accs[g][:], func=SIGMOID, bias=lower[:], scale=-1.0)
+            nc.scalar.activation(out=below_upper[:], in_=accs[g][:], func=SIGMOID, bias=upper, scale=-1.0)
+            nc.scalar.activation(out=below_lower[:], in_=accs[g][:], func=SIGMOID, bias=lower, scale=-1.0)
             result = pool.tile([P, GROUP], F32, name="result%d" % g)
             nc.vector.tensor_tensor(out=result[:], in0=below_upper[:], in1=below_lower[:], op=SUBTRACT)
             nc.sync.dma_start(out=out[0, :, g * GROUP : (g + 1) * GROUP], in_=result[:])
 
-        gather_words(0)
-        gather_words(1)
+        nc.vector.tensor_copy(pairs[:], words[:].bitcast(U32).indirect(offsets[:]))
         cast_q(nc.scalar.copy, 0, 0, NQ)
         cast_q(nc.vector.tensor_copy, 1, 0, VECTOR_COLS)
         cast_q(nc.scalar.copy, 1, VECTOR_COLS, NQ)
         part_words(0)
         quantize_q(0)
         quantize_q(1)
-        for g in range(1, N // GROUP):
-            part_words(g)
+        part_words(1)
+        part_words(2)
+        nc.vector.transpose(thresholds[:], threshold_rows[:])
+        part_words(3)
         for g in range(N // GROUP):
             for o in range(PASSES):
                 multiply(g, o)

@@ -22,7 +22,7 @@ K_PASS = P * PACK
 PASSES = D // K_PASS
 HALF = N // 2
 GROUP = 128
-VECTOR_COLS = 48
+VECTOR_COLS = 64
 Q_BYTES = PACK * NQ * 4
 
 
@@ -127,8 +127,8 @@ def tile_attend_link_ordinal_topk_kernel(tc, qT, k_words, k_scales, c1, c2, offs
         cast_q(nc.scalar.copy, 0, 0, NQ)
         cast_q(nc.vector.tensor_copy, 1, 0, VECTOR_COLS)
         cast_q(nc.scalar.copy, 1, VECTOR_COLS, NQ)
-        part_words(0)
         quantize_q(0)
+        part_words(0)
         quantize_q(1)
         part_words(1)
         part_words(2)

@@ -51,8 +51,8 @@ def tile_attend_link_ordinal_topk_kernel(tc, qT, k_words, k_scales, c1, c2, offs
             nc.sync.dma_start(out=q_raw[o][:], in_=rows.rearrange("(p j) n -> p j n", j=PACK))
         threshold_rows = pool.tile([P, 32], F32, name="threshold_rows", align_bytes=64)
         nc.vector.memset(threshold_rows[:], 0.0)
-        for r, c in enumerate((c2, c1)):
-            nc.scalar.dma_start(out=threshold_rows[r:P:32, :], in_=c[0].rearrange("(q j) o -> q (j o)", j=32))
+        for r, (c, queue) in enumerate(((c2, nc.scalar), (c1, nc.sync))):
+            queue.dma_start(out=threshold_rows[r:P:32, :], in_=c[0].rearrange("(q j) o -> q (j o)", j=32))
         nc.vector.memset(scale_rows[32:64, :].bitcast(I32), 0)
         nc.vector.memset(scale_rows[64:P, :].bitcast(I32), 0)
         key_scales = pool.tile([P, PASSES * N], U8, name="key_scales", align_bytes=64)
@@ -67,7 +67,7 @@ def tile_attend_link_ordinal_topk_kernel(tc, qT, k_words, k_scales, c1, c2, offs
         listed_rows = pool.tile([P, N], U8, name="listed_rows", align_bytes=64)
         nc.vector.tensor_copy(listed_rows[:], scale_rows[:].indirect(offsets[:]))
         for quad in range(4):
-            (nc.sync if quad % 2 == 0 else nc.scalar).dma_start(
+            nc.sync.dma_start(
                 out=key_scales[32 * quad : 32 * quad + 4, :].bitcast(I32).rearrange("p (o n) -> p o n", o=PASSES),
                 in_=listed_rows[8 * quad : 8 * quad + 8, :].bitcast(I32),
             )

@@ -22,6 +22,7 @@ K_PASS = P * PACK
 PASSES = D // K_PASS
 HALF = N // 2
 GROUP = 128
+TAIL_CUT = 64
 VECTOR_COLS = 64
 Q_BYTES = PACK * NQ * 4
 
@@ -72,7 +73,10 @@ def tile_attend_link_ordinal_topk_kernel(tc, qT, k_words, k_scales, c1, c2, offs
                 in_=listed_rows[8 * quad : 8 * quad + 8, :].bitcast(I32),
             )
 
-        q_codes = [pool.tile([P, NQ], U32, name="q_codes%d" % o, align_bytes=64) for o in range(PASSES)]
+        q_codes = [
+            pool.tile([P, NQ], U32, name="q_codes0", align_bytes=64),
+            reused.tile([P, NQ], U32, name="q_codes1", offset=Q_BYTES + GROUP * 4, align_bytes=64),
+        ]
         q_scales = [pool.tile([P, NQ], U8, name="q_scales%d" % o, align_bytes=64) for o in range(PASSES)]
 
         grouped = [pool.tile([P, NQ, PACK], BF16, name="q_grouped%d" % o, align_bytes=64) for o in range(PASSES)]
@@ -83,11 +87,11 @@ def tile_attend_link_ordinal_topk_kernel(tc, qT, k_words, k_scales, c1, c2, offs
                 in_=q_raw[o][:, :, c0:c1].rearrange("p t (c i) -> p c t i", i=4),
             )
 
-        def quantize_q(o):
+        def quantize_q(o, c0, c1):
             nc.vector.quantize_mx(
-                out=q_codes[o][:].bitcast(FP8X4),
-                scales=q_scales[o][:],
-                in_=grouped[o][:].rearrange("p n t -> p (n t)"),
+                out=q_codes[o][:, c0:c1].bitcast(FP8X4),
+                scales=q_scales[o][:, c0:c1],
+                in_=grouped[o][:, c0:c1, :].rearrange("p n t -> p (n t)"),
             )
 
         pairs = pool.tile([P, N], U32, name="pairs", align_bytes=64)
@@ -116,20 +120,23 @@ def tile_attend_link_ordinal_topk_kernel(tc, qT, k_words, k_scales, c1, c2, offs
 
         def link(g):
             below_upper = pool.tile([P, GROUP], F32, name="below_upper%d" % g)
-            below_lower = pool.tile([P, GROUP], F32, name="below_lower%d" % g)
-            nc.scalar.activation(out=below_upper[:], in_=accs[g][:], func=SIGMOID, bias=upper, scale=-1.0)
-            nc.scalar.activation(out=below_lower[:], in_=accs[g][:], func=SIGMOID, bias=lower, scale=-1.0)
             result = pool.tile([P, GROUP], F32, name="result%d" % g)
-            nc.vector.tensor_tensor(out=result[:], in0=below_upper[:], in1=below_lower[:], op=SUBTRACT)
+            nc.scalar.activation(out=below_upper[:], in_=accs[g][:], func=SIGMOID, bias=upper, scale=-1.0)
+            cuts = (0, TAIL_CUT, GROUP) if g == N // GROUP - 1 else (0, GROUP)
+            for a, b in zip(cuts, cuts[1:]):
+                below_lower = pool.tile([P, b - a], F32, name="below_lower%d_%d" % (g, a))
+                nc.scalar.activation(out=below_lower[:], in_=accs[g][:, a:b], func=SIGMOID, bias=lower, scale=-1.0)
+                nc.vector.tensor_tensor(out=result[:, a:b], in0=below_upper[:, a:b], in1=below_lower[:], op=SUBTRACT)
             nc.sync.dma_start(out=out[0, :, g * GROUP : (g + 1) * GROUP], in_=result[:])
 
         nc.vector.tensor_copy(pairs[:], words[:].bitcast(U32).indirect(offsets[:]))
         cast_q(nc.scalar.copy, 0, 0, NQ)
         cast_q(nc.vector.tensor_copy, 1, 0, VECTOR_COLS)
         cast_q(nc.scalar.copy, 1, VECTOR_COLS, NQ)
-        quantize_q(0)
+        quantize_q(0, 0, NQ)
         part_words(0)
-        quantize_q(1)
+        quantize_q(1, 0, VECTOR_COLS)
+        quantize_q(1, VECTOR_COLS, NQ)
         part_words(1)
         part_words(2)
         nc.vector.transpose(thresholds[:], threshold_rows[:])

@@ -83,8 +83,8 @@ def tile_attend_link_ordinal_topk_kernel(tc, qT, k_words, k_scales, c1, c2, offs
 
         def cast_q(copy, o, c0, c1):
             copy(
-                out=grouped[o][:, c0:c1, :].rearrange("p (c i) t -> p c t i", i=4),
-                in_=q_raw[o][:, :, c0:c1].rearrange("p t (c i) -> p c t i", i=4),
+                out=grouped[o][:, c0:c1, :].rearrange("p (c i) t -> p c t i", i=2),
+                in_=q_raw[o][:, :, c0:c1].rearrange("p t (c i) -> p c t i", i=2),
             )
 
         def quantize_q(o, c0, c1):

@@ -50,10 +50,10 @@ def tile_attend_link_ordinal_topk_kernel(tc, qT, k_words, k_scales, c1, c2, offs
         for o in range(PASSES):
             rows = qT[0, o * K_PASS : (o + 1) * K_PASS, :]
             nc.sync.dma_start(out=q_raw[o][:], in_=rows.rearrange("(p j) n -> p j n", j=PACK))
-        threshold_rows = pool.tile([P, 32], F32, name="threshold_rows", align_bytes=64)
-        nc.vector.memset(threshold_rows[:], 0.0)
-        for r, (c, queue) in enumerate(((c2, nc.scalar), (c1, nc.sync))):
-            queue.dma_start(out=threshold_rows[r:P:32, :], in_=c[0].rearrange("(q j) o -> q (j o)", j=32))
+        upper = pool.tile([P, 1], F32, name="upper")
+        lower = pool.tile([P, 1], F32, name="lower")
+        nc.sync.dma_start(out=upper[:], in_=c2[0])
+        nc.sync.dma_start(out=lower[:], in_=c1[0])
         nc.vector.memset(scale_rows[32:64, :].bitcast(I32), 0)
         nc.vector.memset(scale_rows[64:P, :].bitcast(I32), 0)
         key_scales = pool.tile([P, PASSES * N], U8, name="key_scales", align_bytes=64)
@@ -63,8 +63,6 @@ def tile_attend_link_ordinal_topk_kernel(tc, qT, k_words, k_scales, c1, c2, offs
         warmed = pool.tile([P, 1], F32, name="warmed")
         nc.scalar.activation(out=warmed[:], in_=warm[:], func=SIGMOID)
 
-        thresholds = reused.tile([P, 32], F32, name="thresholds", offset=3 * GROUP * 4, align_bytes=64)
-        upper, lower = thresholds[:, 0:1], thresholds[:, 1:2]
         listed_rows = pool.tile([P, N], U8, name="listed_rows", align_bytes=64)
         nc.vector.tensor_copy(listed_rows[:], scale_rows[:].indirect(offsets[:]))
         for quad in range(4):
@@ -121,11 +119,11 @@ def tile_attend_link_ordinal_topk_kernel(tc, qT, k_words, k_scales, c1, c2, offs
         def link(g):
             below_upper = pool.tile([P, GROUP], F32, name="below_upper%d" % g)
             result = pool.tile([P, GROUP], F32, name="result%d" % g)
-            nc.scalar.activation(out=below_upper[:], in_=accs[g][:], func=SIGMOID, bias=upper, scale=-1.0)
+            nc.scalar.activation(out=below_upper[:], in_=accs[g][:], func=SIGMOID, bias=upper[:], scale=-1.0)
             cuts = (0, TAIL_CUT, GROUP) if g == N // GROUP - 1 else (0, GROUP)
             for a, b in zip(cuts, cuts[1:]):
                 below_lower = pool.tile([P, b - a], F32, name="below_lower%d_%d" % (g, a))
-                nc.scalar.activation(out=below_lower[:], in_=accs[g][:, a:b], func=SIGMOID, bias=lower, scale=-1.0)
+                nc.scalar.activation(out=below_lower[:], in_=accs[g][:, a:b], func=SIGMOID, bias=lower[:], scale=-1.0)
                 nc.vector.tensor_tensor(out=result[:, a:b], in0=below_upper[:, a:b], in1=below_lower[:], op=SUBTRACT)
             nc.sync.dma_start(out=out[0, :, g * GROUP : (g + 1) * GROUP], in_=result[:])
 
@@ -139,7 +137,6 @@ def tile_attend_link_ordinal_topk_kernel(tc, qT, k_words, k_scales, c1, c2, offs
         quantize_q(1, VECTOR_COLS, NQ)
         part_words(1)
         part_words(2)
-        nc.vector.transpose(thresholds[:], threshold_rows[:])
         part_words(3)
         for g in range(N // GROUP):
             for o in range(PASSES):

@@ -20,10 +20,10 @@ P = 128
 PACK = 4
 K_PASS = P * PACK
 PASSES = D // K_PASS
-HALF = N // 2
 GROUP = 128
+GATHERS = ((0, 128), (128, 384), (384, 512))
 TAIL_CUT = 64
-VECTOR_COLS = 64
+VECTOR_QUERIES = 64
 Q_BYTES = PACK * NQ * 4
 
 
@@ -36,17 +36,11 @@ def tile_attend_link_ordinal_topk_kernel(tc, qT, k_words, k_scales, c1, c2, offs
 
         offsets = pool.tile([P, N // 16], U16, name="offsets")
         scale_rows = pool.tile([P, T], U8, name="scale_rows", align_bytes=64)
-        nc.sync.dma_start(
-            out=scale_rows[0:32, :].bitcast(I32),
-            in_=k_scales.bitcast(I32).rearrange("o f t -> f o t"),
-        )
+        nc.sync.dma_start(out=scale_rows[0:32, :].bitcast(I32), in_=k_scales.bitcast(I32).rearrange("o f t -> f o t"))
         nc.sync.dma_start(offsets[:], offs)
-        q_raw = [
-            reused.tile([P, PACK, NQ], F32, name="q_raw0", offset=Q_BYTES, align_bytes=64),
-            reused.tile([P, PACK, NQ], F32, name="q_raw1", offset=0, align_bytes=64),
-        ]
         words = pool.tile([P, T], I32, name="words", align_bytes=64)
         nc.sync.dma_start(out=words[:], in_=k_words[0].rearrange("g t b -> g (t b)").bitcast(I32))
+        q_raw = [reused.tile([P, PACK, NQ], F32, name="q_raw%d" % o, offset=o * Q_BYTES, align_bytes=64) for o in range(PASSES)]
         for o in range(PASSES):
             rows = qT[0, o * K_PASS : (o + 1) * K_PASS, :]
             nc.sync.dma_start(out=q_raw[o][:], in_=rows.rearrange("(p j) n -> p j n", j=PACK))
@@ -54,6 +48,7 @@ def tile_attend_link_ordinal_topk_kernel(tc, qT, k_words, k_scales, c1, c2, offs
         lower = pool.tile([P, 1], F32, name="lower")
         nc.sync.dma_start(out=upper[:], in_=c2[0])
         nc.sync.dma_start(out=lower[:], in_=c1[0])
+
         nc.vector.memset(scale_rows[32:64, :].bitcast(I32), 0)
         nc.vector.memset(scale_rows[64:P, :].bitcast(I32), 0)
         key_scales = pool.tile([P, PASSES * N], U8, name="key_scales", align_bytes=64)
@@ -66,17 +61,13 @@ def tile_attend_link_ordinal_topk_kernel(tc, qT, k_words, k_scales, c1, c2, offs
         listed_rows = pool.tile([P, N], U8, name="listed_rows", align_bytes=64)
         nc.vector.tensor_copy(listed_rows[:], scale_rows[:].indirect(offsets[:]))
         for quad in range(4):
-            nc.sync.dma_start(
+            nc.scalar.dma_start(
                 out=key_scales[32 * quad : 32 * quad + 4, :].bitcast(I32).rearrange("p (o n) -> p o n", o=PASSES),
                 in_=listed_rows[8 * quad : 8 * quad + 8, :].bitcast(I32),
             )
 
-        q_codes = [
-            pool.tile([P, NQ], U32, name="q_codes0", align_bytes=64),
-            reused.tile([P, NQ], U32, name="q_codes1", offset=Q_BYTES + GROUP * 4, align_bytes=64),
-        ]
+        q_codes = [pool.tile([P, NQ], U32, name="q_codes%d" % o, align_bytes=64) for o in range(PASSES)]
         q_scales = [pool.tile([P, NQ], U8, name="q_scales%d" % o, align_bytes=64) for o in range(PASSES)]
-
         grouped = [pool.tile([P, NQ, PACK], BF16, name="q_grouped%d" % o, align_bytes=64) for o in range(PASSES)]
 
         def cast_q(copy, o, c0, c1):
@@ -92,54 +83,70 @@ def tile_attend_link_ordinal_topk_kernel(tc, qT, k_words, k_scales, c1, c2, offs
                 in_=grouped[o][:, c0:c1, :].rearrange("p n t -> p (n t)"),
             )
 
-        pairs = pool.tile([P, N], U32, name="pairs", align_bytes=64)
-        pieces = [(g * GROUP, (g + 1) * GROUP, (g - 1) * GROUP * 4 if g else Q_BYTES) for g in range(N // GROUP)]
-        key_codes = [
-            reused.tile([P, PASSES, b - a], U16, name="key_codes%d" % a, offset=at, align_bytes=64) for a, b, at in pieces
+        pairs = [
+            pool.tile([P, 128], U32, name="pairs0", align_bytes=64),
+            pool.tile([P, 256], U32, name="pairs1", align_bytes=64),
+            reused.tile([P, 128], U32, name="pairs2", offset=Q_BYTES, align_bytes=64),
         ]
+        group_pairs = [pairs[0][:], pairs[1][:, 0:GROUP], pairs[1][:, GROUP:], pairs[2][:]]
+        first_codes = pool.tile([P, PASSES, GROUP], U16, name="first_codes", align_bytes=64)
+        held_at = {(1, 0): 0, (1, 1): Q_BYTES + 512, (2, 0): Q_BYTES + 768, (2, 1): Q_BYTES + 1024}
+        key_codes = {(0, o): first_codes[:, o, :] for o in range(PASSES)}
+        for (g, o), at in held_at.items():
+            key_codes[g, o] = reused.tile([P, GROUP], U16, name="codes%d_%d" % (g, o), offset=at, align_bytes=64)[:]
+        for o in range(PASSES):
+            key_codes[3, o] = pool.tile([P, GROUP], U16, name="codes3_%d" % o, align_bytes=64)[:]
 
-        def part_words(i):
-            a, b = pieces[i][:2]
-            nc.vector.tensor_copy(key_codes[i][:], pairs[:, a:b].bitcast(U16).rearrange("p (n o) -> p o n", o=PASSES))
+        def gather(g):
+            a, b = GATHERS[g]
+            nc.vector.tensor_copy(pairs[g][:], words[:].bitcast(U32).indirect(offsets[:, a // 16 : b // 16]))
+
+        def part(g, o):
+            nc.vector.tensor_copy(key_codes[g, o], group_pairs[g].bitcast(U16)[:, o::PASSES])
 
         accs = [psum.tile([P, GROUP], F32, name="acc%d" % g) for g in range(N // GROUP)]
 
         def multiply(g, o):
-            s0 = o * N + g * GROUP
+            a, b = g * GROUP, (g + 1) * GROUP
             nc.tensor.matmul_mx(
                 out=accs[g][:],
                 lhsT=q_codes[o][:].bitcast(FP8X4),
                 lhsT_scale=q_scales[o][:],
-                rhs=key_codes[g][:, o, :].bitcast(FP4X4),
-                rhs_scale=key_scales[:, s0 : s0 + GROUP],
+                rhs=key_codes[g, o].bitcast(FP4X4),
+                rhs_scale=key_scales[:, o * N + a : o * N + b],
                 start=(o == 0),
                 stop=(o == PASSES - 1),
             )
 
         def link(g):
-            below_upper = pool.tile([P, GROUP], F32, name="below_upper%d" % g)
-            result = pool.tile([P, GROUP], F32, name="result%d" % g)
+            a, b = g * GROUP, (g + 1) * GROUP
+            below_upper = pool.tile([P, b - a], F32, name="below_upper%d" % g)
+            result = pool.tile([P, b - a], F32, name="result%d" % g)
             nc.scalar.activation(out=below_upper[:], in_=accs[g][:], func=SIGMOID, bias=upper[:], scale=-1.0)
-            cuts = (0, TAIL_CUT, GROUP) if g == N // GROUP - 1 else (0, GROUP)
-            for a, b in zip(cuts, cuts[1:]):
-                below_lower = pool.tile([P, b - a], F32, name="below_lower%d_%d" % (g, a))
-                nc.scalar.activation(out=below_lower[:], in_=accs[g][:, a:b], func=SIGMOID, bias=lower[:], scale=-1.0)
-                nc.vector.tensor_tensor(out=result[:, a:b], in0=below_upper[:, a:b], in1=below_lower[:], op=SUBTRACT)
-            nc.sync.dma_start(out=out[0, :, g * GROUP : (g + 1) * GROUP], in_=result[:])
+            cuts = (0, GROUP - TAIL_CUT, GROUP) if b == N else (0, GROUP)
+            for lo, hi in zip(cuts, cuts[1:]):
+                below_lower = pool.tile([P, hi - lo], F32, name="below_lower%d_%d" % (g, lo))
+                nc.scalar.activation(out=below_lower[:], in_=accs[g][:, lo:hi], func=SIGMOID, bias=lower[:], scale=-1.0)
+                nc.vector.tensor_tensor(out=result[:, lo:hi], in0=below_upper[:, lo:hi], in1=below_lower[:], op=SUBTRACT)
+            nc.sync.dma_start(out=out[0, :, a:b], in_=result[:])
 
-        nc.vector.tensor_copy(pairs[:], words[:].bitcast(U32).indirect(offsets[:]))
+        gather(0)
+        gather(1)
+        nc.vector.tensor_copy(first_codes[:], pairs[0][:].bitcast(U16).rearrange("p (n o) -> p o n", o=PASSES))
         cast_q(nc.scalar.copy, 0, 0, NQ)
-        cast_q(nc.vector.tensor_copy, 1, 0, VECTOR_COLS)
-        cast_q(nc.scalar.copy, 1, VECTOR_COLS, NQ)
+        cast_q(nc.vector.tensor_copy, 1, 0, VECTOR_QUERIES)
+        cast_q(nc.scalar.copy, 1, VECTOR_QUERIES, NQ)
         quantize_q(0, 0, NQ)
-        part_words(0)
-        quantize_q(1, 0, VECTOR_COLS)
-        quantize_q(1, VECTOR_COLS, NQ)
-        part_words(1)
-        part_words(2)
-        part_words(3)
-        for g in range(N // GROUP):
-            for o in range(PASSES):
-                multiply(g, o)
+        part(1, 0)
+        quantize_q(1, 0, NQ // 2)
+        quantize_q(1, NQ // 2, NQ)
+        part(1, 1)
+        gather(2)
+        part(2, 0)
+        part(2, 1)
+        part(3, 0)
+        part(3, 1)
+        for g, o in ((0, 0), (1, 0), (0, 1), (1, 1), (2, 0), (2, 1), (3, 0), (3, 1)):
+            multiply(g, o)
         for g in range(N // GROUP):
             link(g)

@@ -146,7 +146,8 @@ def tile_attend_link_ordinal_topk_kernel(tc, qT, k_words, k_scales, c1, c2, offs
         part(2, 1)
         part(3, 0)
         part(3, 1)
-        for g, o in ((0, 0), (1, 0), (0, 1), (1, 1), (2, 0), (2, 1), (3, 0), (3, 1)):
-            multiply(g, o)
+        for g in range(N // GROUP):
+            for o in range(PASSES):
+                multiply(g, o)
         for g in range(N // GROUP):
             link(g)

from contextlib import ExitStack

import concourse.mybir as mybir

D, T, N, NQ = 1024, 2048, 512, 128
FLOPS = 2 * D * N * NQ

F32 = mybir.dt.float32
BF16 = mybir.dt.bfloat16
I32 = mybir.dt.int32
U32 = mybir.dt.uint32
U16 = mybir.dt.uint16
U8 = mybir.dt.uint8
FP8X4 = mybir.dt.float8_e4m3fn_x4
FP4X4 = mybir.dt.float4_e2m1fn_x4
SIGMOID = mybir.ActivationFunctionType.Sigmoid
SUBTRACT = mybir.AluOpType.subtract

P = 128
PACK = 4
K_PASS = P * PACK
PASSES = D // K_PASS
GROUP = 128
GATHERS = ((0, 128), (128, 384), (384, 512))
TAIL_CUT = 64
VECTOR_QUERIES = 64
Q_BYTES = PACK * NQ * 4


def tile_attend_link_ordinal_topk_kernel(tc, qT, k_words, k_scales, c1, c2, offs, out):
    nc = tc.nc
    with ExitStack() as ctx:
        pool = ctx.enter_context(tc.tile_pool(name="held", bufs=1))
        reused = ctx.enter_context(tc.tile_pool(name="reused", bufs=1))
        psum = ctx.enter_context(tc.psum_pool(name="psum", bufs=1))

        offsets = pool.tile([P, N // 16], U16, name="offsets")
        scale_rows = pool.tile([P, T], U8, name="scale_rows", align_bytes=64)
        nc.sync.dma_start(out=scale_rows[0:32, :].bitcast(I32), in_=k_scales.bitcast(I32).rearrange("o f t -> f o t"))
        nc.sync.dma_start(offsets[:], offs)
        words = pool.tile([P, T], I32, name="words", align_bytes=64)
        nc.sync.dma_start(out=words[:], in_=k_words[0].rearrange("g t b -> g (t b)").bitcast(I32))
        q_raw = [reused.tile([P, PACK, NQ], F32, name="q_raw%d" % o, offset=o * Q_BYTES, align_bytes=64) for o in range(PASSES)]
        for o in range(PASSES):
            rows = qT[0, o * K_PASS : (o + 1) * K_PASS, :]
            nc.sync.dma_start(out=q_raw[o][:], in_=rows.rearrange("(p j) n -> p j n", j=PACK))
        upper = pool.tile([P, 1], F32, name="upper")
        lower = pool.tile([P, 1], F32, name="lower")
        nc.sync.dma_start(out=upper[:], in_=c2[0])
        nc.sync.dma_start(out=lower[:], in_=c1[0])

        nc.vector.memset(scale_rows[32:64, :].bitcast(I32), 0)
        nc.vector.memset(scale_rows[64:P, :].bitcast(I32), 0)
        key_scales = pool.tile([P, PASSES * N], U8, name="key_scales", align_bytes=64)
        nc.vector.memset(key_scales[:].bitcast(I32), 0)
        warm = pool.tile([P, 1], F32, name="warm")
        nc.vector.memset(warm[:], 0.0)
        warmed = pool.tile([P, 1], F32, name="warmed")
        nc.scalar.activation(out=warmed[:], in_=warm[:], func=SIGMOID)

        listed_rows = pool.tile([P, N], U8, name="listed_rows", align_bytes=64)
        nc.vector.tensor_copy(listed_rows[:], scale_rows[:].indirect(offsets[:]))
        for quad in range(4):
            nc.scalar.dma_start(
                out=key_scales[32 * quad : 32 * quad + 4, :].bitcast(I32).rearrange("p (o n) -> p o n", o=PASSES),
                in_=listed_rows[8 * quad : 8 * quad + 8, :].bitcast(I32),
            )

        q_codes = [pool.tile([P, NQ], U32, name="q_codes%d" % o, align_bytes=64) for o in range(PASSES)]
        q_scales = [pool.tile([P, NQ], U8, name="q_scales%d" % o, align_bytes=64) for o in range(PASSES)]
        grouped = [pool.tile([P, NQ, PACK], BF16, name="q_grouped%d" % o, align_bytes=64) for o in range(PASSES)]

        def cast_q(copy, o, c0, c1):
            copy(
                out=grouped[o][:, c0:c1, :].rearrange("p (c i) t -> p c t i", i=2),
                in_=q_raw[o][:, :, c0:c1].rearrange("p t (c i) -> p c t i", i=2),
            )

        def quantize_q(o, c0, c1):
            nc.vector.quantize_mx(
                out=q_codes[o][:, c0:c1].bitcast(FP8X4),
                scales=q_scales[o][:, c0:c1],
                in_=grouped[o][:, c0:c1, :].rearrange("p n t -> p (n t)"),
            )

        pairs = [
            pool.tile([P, 128], U32, name="pairs0", align_bytes=64),
            pool.tile([P, 256], U32, name="pairs1", align_bytes=64),
            reused.tile([P, 128], U32, name="pairs2", offset=Q_BYTES, align_bytes=64),
        ]
        group_pairs = [pairs[0][:], pairs[1][:, 0:GROUP], pairs[1][:, GROUP:], pairs[2][:]]
        first_codes = pool.tile([P, PASSES, GROUP], U16, name="first_codes", align_bytes=64)
        held_at = {(1, 0): 0, (1, 1): Q_BYTES + 512, (2, 0): Q_BYTES + 768, (2, 1): Q_BYTES + 1024}
        key_codes = {(0, o): first_codes[:, o, :] for o in range(PASSES)}
        for (g, o), at in held_at.items():
            key_codes[g, o] = reused.tile([P, GROUP], U16, name="codes%d_%d" % (g, o), offset=at, align_bytes=64)[:]
        for o in range(PASSES):
            key_codes[3, o] = pool.tile([P, GROUP], U16, name="codes3_%d" % o, align_bytes=64)[:]

        def gather(g):
            a, b = GATHERS[g]
            nc.vector.tensor_copy(pairs[g][:], words[:].bitcast(U32).indirect(offsets[:, a // 16 : b // 16]))

        def part(g, o):
            nc.vector.tensor_copy(key_codes[g, o], group_pairs[g].bitcast(U16)[:, o::PASSES])

        accs = [psum.tile([P, GROUP], F32, name="acc%d" % g) for g in range(N // GROUP)]

        def multiply(g, o):
            a, b = g * GROUP, (g + 1) * GROUP
            nc.tensor.matmul_mx(
                out=accs[g][:],
                lhsT=q_codes[o][:].bitcast(FP8X4),
                lhsT_scale=q_scales[o][:],
                rhs=key_codes[g, o].bitcast(FP4X4),
                rhs_scale=key_scales[:, o * N + a : o * N + b],
                start=(o == 0),
                stop=(o == PASSES - 1),
            )

        def link(g):
            a, b = g * GROUP, (g + 1) * GROUP
            below_upper = pool.tile([P, b - a], F32, name="below_upper%d" % g)
            result = pool.tile([P, b - a], F32, name="result%d" % g)
            nc.scalar.activation(out=below_upper[:], in_=accs[g][:], func=SIGMOID, bias=upper[:], scale=-1.0)
            cuts = (0, GROUP - TAIL_CUT, GROUP) if b == N else (0, GROUP)
            for lo, hi in zip(cuts, cuts[1:]):
                below_lower = pool.tile([P, hi - lo], F32, name="below_lower%d_%d" % (g, lo))
                nc.scalar.activation(out=below_lower[:], in_=accs[g][:, lo:hi], func=SIGMOID, bias=lower[:], scale=-1.0)
                nc.vector.tensor_tensor(out=result[:, lo:hi], in0=below_upper[:, lo:hi], in1=below_lower[:], op=SUBTRACT)
            nc.sync.dma_start(out=out[0, :, a:b], in_=result[:])

        gather(0)
        gather(1)
        nc.vector.tensor_copy(first_codes[:], pairs[0][:].bitcast(U16).rearrange("p (n o) -> p o n", o=PASSES))
        cast_q(nc.scalar.copy, 0, 0, NQ)
        cast_q(nc.vector.tensor_copy, 1, 0, VECTOR_QUERIES)
        cast_q(nc.scalar.copy, 1, VECTOR_QUERIES, NQ)
        quantize_q(0, 0, NQ)
        part(1, 0)
        quantize_q(1, 0, NQ // 2)
        quantize_q(1, NQ // 2, NQ)
        part(1, 1)
        gather(2)
        part(2, 0)
        part(2, 1)
        part(3, 0)
        part(3, 1)
        for g in range(N // GROUP):
            for o in range(PASSES):
                multiply(g, o)
        for g in range(N // GROUP):
            link(g)
